import numpy as np
import ml_dtypes


def mxq(x, axis, fmt="e4m3"):
    dtype, down = {"e4m3": (ml_dtypes.float8_e4m3fn, 7), "e5m2": (ml_dtypes.float8_e5m2, 14)}[fmt]
    v = np.moveaxis(np.asarray(x, np.float32).astype(ml_dtypes.bfloat16).astype(np.float64), axis, -1)
    blocks = v.reshape(v.shape[:-1] + (-1, 32))
    amax = np.abs(blocks).max(-1, keepdims=True)
    byte = np.maximum(np.where(amax > 0, np.frexp(amax)[1] - 1 + 127, 0) - down, 1)
    scale = np.exp2(byte - 127.0)
    codes = (blocks / scale).astype(np.float32).astype(dtype).astype(np.float64)
    return np.moveaxis((codes * scale).reshape(v.shape), -1, axis)


WIDE = False


def mx_kscale(k):
    if not WIDE:
        return np.ones(k)
    levels = np.array([10, -10, 5, -5, 0])
    if k % 512:
        return np.exp2(np.random.permutation(np.resize(levels, k // 32))).repeat(32)
    a = np.empty((k // 512, 16))
    for p in range(k // 512):
        a[p, :8] = np.random.permutation(np.resize(levels, 8))
        for g in range(8):
            far = levels[np.abs(levels - a[p, g]) >= 10]
            a[p, g + 8] = far[np.random.randint(len(far))]
    return np.exp2(a.ravel()).repeat(32)


def f64(x):
    return np.asarray(x).astype(np.float64)


def striped(idx):
    return np.tile(idx.reshape(-1, 16).T, (8, 1)).astype(np.uint16)


def unstriped(offs):
    return offs[:16].T.reshape(-1).astype(np.int64)


def pack_weight(w):
    k, n = w.shape
    w = f64(np.asarray(w, np.float32).astype(ml_dtypes.bfloat16)).reshape(k // 32, 32, n)
    amax = np.abs(w).max(1)
    byte = np.clip(np.where(amax > 0, np.frexp(amax)[1] - 1 + 127 - 7, 1), 1, 254)
    scaled = (w * np.exp2(127.0 - byte)[:, None, :]).reshape(k, n).astype(np.float32)
    words = np.ascontiguousarray(scaled.reshape(k // 512, 128, 4, n).transpose(0, 1, 3, 2)).astype(ml_dtypes.float8_e4m3fn).view(np.uint8)
    return words, np.ascontiguousarray(byte.astype(np.uint8).reshape(k // 512, 16, n))


def unpack_weight(words, scales):
    g, p, n, _ = words.shape
    vals = np.ascontiguousarray(words).view(ml_dtypes.float8_e4m3fn).astype(np.float64) * np.repeat(np.exp2(scales.astype(np.float64) - 127.0), 8, axis=1)[..., None]
    return vals.transpose(0, 1, 3, 2).reshape(g * 512, n)


def relu(v):
    return np.maximum(v, 0.0)


K, T, S, V, H, N = 512, 4096, 1024, 512, 512, 256


def setup_inputs():
    n = np.random.standard_normal
    s = mx_kscale(K)[:, None]
    u = mx_kscale(H)
    packed_w2 = pack_weight(n((H, N)) / np.sqrt(H) / u[:, None])
    return {
        "xT": (n((K, T)) * s).astype(np.float32),
        "w1": (n((K, H)) / np.sqrt(K) / s * u).astype(np.float32),
        "w2_words": packed_w2[0],
        "w2_scales": packed_w2[1],
        "offs": striped(np.random.permutation(T)[:S]),
    }


def reference(xT, w1, w2_words, w2_scales, offs):
    xq = mxq(f64(xT)[:, unstriped(offs)], 0, "e4m3")
    h = relu(mxq(f64(w1), 0, "e4m3").T @ xq)
    z = np.abs(h[:, :V] - h[:, V:2 * V])
    return unpack_weight(w2_words, w2_scales).T @ mxq(z, 0, "e4m3")

@@ -1,0 +1,137 @@
+from contextlib import ExitStack
+
+import concourse.mybir as mybir
+
+K, T, S, V, H, N = 512, 4096, 1024, 512, 512, 256
+FLOPS = 2 * K * H * S + 2 * H * N * V
+
+F32 = mybir.dt.float32
+BF16 = mybir.dt.bfloat16
+I32 = mybir.dt.int32
+U32 = mybir.dt.uint32
+U16 = mybir.dt.uint16
+U8 = mybir.dt.uint8
+FP8X4 = mybir.dt.float8_e4m3fn_x4
+ALU = mybir.AluOpType
+ACT = mybir.ActivationFunctionType
+
+P = 128
+PACK = 4
+PAIRS = 128
+CHUNKS = V // PAIRS
+W_PARTS = 2
+ABS_ON_SCALAR = (0, 1)
+
+
+def tile_picked_siam_abs_e_kernel(tc, xT, w1, w2_words, w2_scales, offs, out):
+    nc = tc.nc
+    with ExitStack() as ctx:
+        keep = ctx.enter_context(tc.tile_pool(name="keep", bufs=1))
+        psum = ctx.enter_context(tc.psum_pool(name="psum", bufs=1))
+
+        offsets = keep.tile([P, S // 16], U16, name="offsets")
+
+        w2_codes = keep.tile([P, N], U32, name="w2_codes", align_bytes=64)
+        w2_plane = keep.tile([P, N], U8, name="w2_plane", align_bytes=64)
+        nc.gpsimd.memset(w2_plane[:].bitcast(I32), 0)
+
+        x_rows = xT.rearrange("(p j) t -> p j t", j=PACK)
+        planes = []
+        for j in range(PACK):
+            plane = keep.tile([P, T], F32, name="plane%d" % j)
+            nc.sync.dma_start(plane[:], x_rows[:, j, :])
+            planes.append(plane)
+            if j == 0:
+                nc.sync.dma_start(offsets[:], offs)
+
+        w1_rows = w1.rearrange("(p j) c -> p j c", j=PACK)
+        cols = H // W_PARTS
+        w1_raw = []
+        for h in range(W_PARTS):
+            raw = keep.tile([P, PACK, cols], F32, name="w1_raw%d" % h)
+            nc.sync.dma_start(raw[:], w1_rows[:, :, h * cols : (h + 1) * cols])
+            w1_raw.append(raw)
+
+        nc.sync.dma_start(w2_codes[:].bitcast(I32), w2_words[0].rearrange("p n t -> p (n t)").bitcast(I32))
+        for q in range(4):
+            nc.sync.dma_start(w2_plane[32 * q : 32 * q + 4, :].bitcast(I32), w2_scales[0, 4 * q : 4 * q + 4, :].bitcast(I32))
+
+        picked = keep.tile([P, CHUNKS, 2, PAIRS, PACK], BF16, name="picked", align_bytes=64)
+        for j in range(PACK):
+            nc.vector.tensor_copy(
+                picked[:, :, :, :, j].rearrange("p c s n -> p s c n"),
+                planes[j][:].indirect(offsets[:]),
+            )
+
+        w1_grouped = keep.tile([P, PACK, P, PACK], BF16, name="w1_grouped", tag="shared", align_bytes=64)
+        ms = cols // PACK
+        for h in range(W_PARTS):
+            nc.scalar.copy(
+                w1_grouped[:, :, h * ms : (h + 1) * ms, :].rearrange("p t m j -> p m j t"),
+                w1_raw[h][:].rearrange("p j (m t) -> p m j t", t=PACK),
+            )
+        w1_codes = keep.tile([P, H], U32, name="w1_codes", align_bytes=64)
+        w1_plane = keep.tile([P, H], U8, name="w1_plane", align_bytes=64)
+        nc.vector.quantize_mx(
+            out=w1_codes[:].bitcast(FP8X4), scales=w1_plane[:], in_=w1_grouped[:].rearrange("p t m j -> p (t m j)")
+        )
+
+        later_codes = keep.tile([P, CHUNKS, 2 * PAIRS], U32, name="later_codes", tag="shared", align_bytes=64)
+        first_codes = keep.tile([P, 2 * PAIRS], U32, name="first_codes", align_bytes=64)
+        out_rows = out.rearrange("(r p) v -> p r v", p=P)
+        for c in range(CHUNKS):
+            x_codes = first_codes[:] if c < 1 else later_codes[:, c, :]
+            x_plane = keep.tile([P, 2 * PAIRS], U8, name="x_plane%d" % c, align_bytes=64)
+            nc.vector.quantize_mx(
+                out=x_codes.bitcast(FP8X4), scales=x_plane[:], in_=picked[:, c].rearrange("p s n j -> p (s n j)")
+            )
+            sides = []
+            for s in range(2):
+                bank = psum.tile([P, PACK, PAIRS], F32, name="hidden%d_%d" % (c, s), tag="bank%d_%d" % (c, s))
+                tokens = slice(s * PAIRS, (s + 1) * PAIRS)
+                for t in range(PACK):
+                    channels = slice(t * P, (t + 1) * P)
+                    nc.tensor.matmul_mx(
+                        out=bank[:, t, :],
+                        lhsT=w1_codes[:, channels].bitcast(FP8X4),
+                        lhsT_scale=w1_plane[:, channels],
+                        rhs=x_codes[:, tokens].bitcast(FP8X4),
+                        rhs_scale=x_plane[:, tokens],
+                        start=True,
+                        stop=True,
+                    )
+                sides.append(bank)
+
+            first = keep.tile([P, PAIRS, PACK], F32, name="first%d" % c)
+            nc.scalar.activation(first[:], sides[0][:].rearrange("p t n -> p n t"), ACT.Relu)
+            diff = keep.tile([P, PAIRS, PACK], BF16, name="diff%d" % c)
+            nc.vector.scalar_tensor_tensor(
+                out=diff[:], in0=sides[1][:].rearrange("p t n -> p n t"), scalar=0.0, in1=first[:], op0=ALU.max, op1=ALU.subtract
+            )
+            z = keep.tile([P, PAIRS * PACK], BF16, name="z%d" % c, align_bytes=64)
+            flat = diff[:].rearrange("p n t -> p (n t)")
+            if c in ABS_ON_SCALAR:
+                nc.scalar.activation(z[:], flat, ACT.Abs)
+            else:
+                negated = keep.tile([P, PAIRS * PACK], BF16, name="negated%d" % c)
+                nc.vector.tensor_scalar(out=negated[:], in0=flat, scalar1=-1.0, scalar2=None, op0=ALU.mult)
+                nc.vector.tensor_tensor(out=z[:], in0=flat, in1=negated[:], op=ALU.max)
+            z_codes = keep.tile([P, PAIRS], U32, name="z_codes%d" % c, align_bytes=64)
+            z_plane = keep.tile([P, PAIRS], U8, name="z_plane%d" % c, align_bytes=64)
+            nc.vector.quantize_mx(out=z_codes[:].bitcast(FP8X4), scales=z_plane[:], in_=z[:])
+
+            result = psum.tile([P, N // P, PAIRS], F32, name="result%d" % c, tag="bank%d_0" % c)
+            for r in range(N // P):
+                rows = slice(r * P, (r + 1) * P)
+                nc.tensor.matmul_mx(
+                    out=result[:, r, :],
+                    lhsT=w2_codes[:, rows].bitcast(FP8X4),
+                    lhsT_scale=w2_plane[:, rows],
+                    rhs=z_codes[:].bitcast(FP8X4),
+                    rhs_scale=z_plane[:],
+                    start=True,
+                    stop=True,
+                )
+            staged = keep.tile([P, N // P, PAIRS], F32, name="staged%d" % c)
+            nc.scalar.copy(staged[:], result[:])
+            nc.sync.dma_start(out_rows[:, :, c * PAIRS : (c + 1) * PAIRS], staged[:])

@@ -20,20 +20,35 @@ PACK = 4
 PAIRS = 128
 CHUNKS = V // PAIRS
 W_PARTS = 2
-ABS_ON_SCALAR = (0, 1)
+WARM_PASSES = 5
+ABS_ON_VECTOR = (0,)
+GROUPS = ((0, 2), (2, 3), (3, 4))
 
 
 def tile_picked_siam_abs_e_kernel(tc, xT, w1, w2_words, w2_scales, offs, out):
     nc = tc.nc
+
+    def mx_pass(acc, lhs_codes, lhs_plane, rhs_codes, rhs_plane):
+        nc.tensor.matmul_mx(
+            out=acc,
+            lhsT=lhs_codes.bitcast(FP8X4),
+            lhsT_scale=lhs_plane,
+            rhs=rhs_codes.bitcast(FP8X4),
+            rhs_scale=rhs_plane,
+            start=True,
+            stop=True,
+        )
+
     with ExitStack() as ctx:
         keep = ctx.enter_context(tc.tile_pool(name="keep", bufs=1))
         psum = ctx.enter_context(tc.psum_pool(name="psum", bufs=1))
 
         offsets = keep.tile([P, S // 16], U16, name="offsets")
-
         w2_codes = keep.tile([P, N], U32, name="w2_codes", align_bytes=64)
         w2_plane = keep.tile([P, N], U8, name="w2_plane", align_bytes=64)
         nc.gpsimd.memset(w2_plane[:].bitcast(I32), 0)
+        for q in range(4):
+            nc.scalar.dma_start(w2_plane[32 * q : 32 * q + 4, :].bitcast(I32), w2_scales[0, 4 * q : 4 * q + 4, :].bitcast(I32))
 
         x_rows = xT.rearrange("(p j) t -> p j t", j=PACK)
         planes = []
@@ -51,10 +66,7 @@ def tile_picked_siam_abs_e_kernel(tc, xT, w1, w2_words, w2_scales, offs, out):
             raw = keep.tile([P, PACK, cols], F32, name="w1_raw%d" % h)
             nc.sync.dma_start(raw[:], w1_rows[:, :, h * cols : (h + 1) * cols])
             w1_raw.append(raw)
-
         nc.sync.dma_start(w2_codes[:].bitcast(I32), w2_words[0].rearrange("p n t -> p (n t)").bitcast(I32))
-        for q in range(4):
-            nc.sync.dma_start(w2_plane[32 * q : 32 * q + 4, :].bitcast(I32), w2_scales[0, 4 * q : 4 * q + 4, :].bitcast(I32))
 
         picked = keep.tile([P, CHUNKS, 2, PAIRS, PACK], BF16, name="picked", align_bytes=64)
         for j in range(PACK):
@@ -76,11 +88,15 @@ def tile_picked_siam_abs_e_kernel(tc, xT, w1, w2_words, w2_scales, offs, out):
             out=w1_codes[:].bitcast(FP8X4), scales=w1_plane[:], in_=w1_grouped[:].rearrange("p t m j -> p (t m j)")
         )
 
+        warm = psum.tile([P, N], F32, name="warm", tag="bank%d_1" % (CHUNKS - 1))
+        for i in range(WARM_PASSES):
+            mx_pass(warm[:], w2_codes[:, :P], w2_plane[:, :P], w2_codes[:], w2_plane[:])
+
         later_codes = keep.tile([P, CHUNKS, 2 * PAIRS], U32, name="later_codes", tag="shared", align_bytes=64)
         first_codes = keep.tile([P, 2 * PAIRS], U32, name="first_codes", align_bytes=64)
-        out_rows = out.rearrange("(r p) v -> p r v", p=P)
+        hidden = []
         for c in range(CHUNKS):
-            x_codes = first_codes[:] if c < 1 else later_codes[:, c, :]
+            x_codes = first_codes[:] if c == 0 else later_codes[:, c, :]
             x_plane = keep.tile([P, 2 * PAIRS], U8, name="x_plane%d" % c, align_bytes=64)
             nc.vector.quantize_mx(
                 out=x_codes.bitcast(FP8X4), scales=x_plane[:], in_=picked[:, c].rearrange("p s n j -> p (s n j)")
@@ -91,47 +107,49 @@ def tile_picked_siam_abs_e_kernel(tc, xT, w1, w2_words, w2_scales, offs, out):
                 tokens = slice(s * PAIRS, (s + 1) * PAIRS)
                 for t in range(PACK):
                     channels = slice(t * P, (t + 1) * P)
-                    nc.tensor.matmul_mx(
-                        out=bank[:, t, :],
-                        lhsT=w1_codes[:, channels].bitcast(FP8X4),
-                        lhsT_scale=w1_plane[:, channels],
-                        rhs=x_codes[:, tokens].bitcast(FP8X4),
-                        rhs_scale=x_plane[:, tokens],
-                        start=True,
-                        stop=True,
-                    )
+                    mx_pass(bank[:, t, :], w1_codes[:, channels], w1_plane[:, channels], x_codes[:, tokens], x_plane[:, tokens])
                 sides.append(bank)
+            hidden.append(sides)
 
+        firsts = []
+        for c in range(CHUNKS):
             first = keep.tile([P, PAIRS, PACK], F32, name="first%d" % c)
-            nc.scalar.activation(first[:], sides[0][:].rearrange("p t n -> p n t"), ACT.Relu)
+            nc.scalar.activation(first[:], hidden[c][0][:].rearrange("p t n -> p n t"), ACT.Relu)
+            firsts.append(first)
+        diffs = []
+        for c in range(CHUNKS):
             diff = keep.tile([P, PAIRS, PACK], BF16, name="diff%d" % c)
             nc.vector.scalar_tensor_tensor(
-                out=diff[:], in0=sides[1][:].rearrange("p t n -> p n t"), scalar=0.0, in1=first[:], op0=ALU.max, op1=ALU.subtract
+                out=diff[:], in0=hidden[c][1][:].rearrange("p t n -> p n t"), scalar=0.0, in1=firsts[c][:], op0=ALU.max, op1=ALU.subtract
             )
-            z = keep.tile([P, PAIRS * PACK], BF16, name="z%d" % c, align_bytes=64)
-            flat = diff[:].rearrange("p n t -> p (n t)")
-            if c in ABS_ON_SCALAR:
-                nc.scalar.activation(z[:], flat, ACT.Abs)
-            else:
+            diffs.append(diff)
+        z = keep.tile([P, CHUNKS, PAIRS * PACK], BF16, name="z", align_bytes=64)
+        for c in range(CHUNKS):
+            flat = diffs[c][:].rearrange("p n t -> p (n t)")
+            if c in ABS_ON_VECTOR:
                 negated = keep.tile([P, PAIRS * PACK], BF16, name="negated%d" % c)
                 nc.vector.tensor_scalar(out=negated[:], in0=flat, scalar1=-1.0, scalar2=None, op0=ALU.mult)
-                nc.vector.tensor_tensor(out=z[:], in0=flat, in1=negated[:], op=ALU.max)
-            z_codes = keep.tile([P, PAIRS], U32, name="z_codes%d" % c, align_bytes=64)
-            z_plane = keep.tile([P, PAIRS], U8, name="z_plane%d" % c, align_bytes=64)
-            nc.vector.quantize_mx(out=z_codes[:].bitcast(FP8X4), scales=z_plane[:], in_=z[:])
+                nc.vector.tensor_tensor(out=z[:, c, :], in0=flat, in1=negated[:], op=ALU.max)
+            else:
+                nc.scalar.activation(z[:, c, :], flat, ACT.Abs)
 
-            result = psum.tile([P, N // P, PAIRS], F32, name="result%d" % c, tag="bank%d_0" % c)
+        results = []
+        for c0, c1 in GROUPS:
+            width = (c1 - c0) * PAIRS
+            z_codes = keep.tile([P, width], U32, name="z_codes%d" % c0, align_bytes=64)
+            z_plane = keep.tile([P, width], U8, name="z_plane%d" % c0, align_bytes=64)
+            nc.vector.quantize_mx(out=z_codes[:].bitcast(FP8X4), scales=z_plane[:], in_=z[:, c0:c1, :].rearrange("p c e -> p (c e)"))
+            halves = []
             for r in range(N // P):
+                result = psum.tile([P, width], F32, name="result%d_%d" % (c0, r), tag="bank%d_%d" % (c0, r))
                 rows = slice(r * P, (r + 1) * P)
-                nc.tensor.matmul_mx(
-                    out=result[:, r, :],
-                    lhsT=w2_codes[:, rows].bitcast(FP8X4),
-                    lhsT_scale=w2_plane[:, rows],
-                    rhs=z_codes[:].bitcast(FP8X4),
-                    rhs_scale=z_plane[:],
-                    start=True,
-                    stop=True,
-                )
-            staged = keep.tile([P, N // P, PAIRS], F32, name="staged%d" % c)
-            nc.scalar.copy(staged[:], result[:])
-            nc.sync.dma_start(out_rows[:, :, c * PAIRS : (c + 1) * PAIRS], staged[:])
+                mx_pass(result[:], w2_codes[:, rows], w2_plane[:, rows], z_codes[:], z_plane[:])
+                halves.append(result)
+            results.append(halves)
+
+        out_rows = out.rearrange("(r p) v -> p r v", p=P)
+        for (c0, c1), halves in zip(GROUPS, results):
+            staged = keep.tile([P, N // P, (c1 - c0) * PAIRS], F32, name="staged%d" % c0)
+            nc.scalar.copy(staged[:, 0, :], halves[0][:])
+            nc.vector.tensor_copy(staged[:, 1, :], halves[1][:])
+            nc.sync.dma_start(out_rows[:, :, c0 * PAIRS : c1 * PAIRS], staged[:])

@@ -19,10 +19,13 @@ P = 128
 PACK = 4
 PAIRS = 128
 CHUNKS = V // PAIRS
-W_PARTS = 2
+CUTS = (0, 1536, 2560, 3584, 4096)
+ROUNDED_ON_VECTOR = (2,)
+QCUTS = ((0, 128), (128, 256), (256, 512))
+OUT_ON_SCALAR = ()
 WARM_PASSES = 5
 ABS_ON_VECTOR = (0,)
-GROUPS = ((0, 2), (2, 3), (3, 4))
+GROUPS = ((0, 1), (1, 2), (2, 3), (3, 4))
 
 
 def tile_picked_siam_abs_e_kernel(tc, xT, w1, w2_words, w2_scales, offs, out):
@@ -51,65 +54,65 @@ def tile_picked_siam_abs_e_kernel(tc, xT, w1, w2_words, w2_scales, offs, out):
             nc.scalar.dma_start(w2_plane[32 * q : 32 * q + 4, :].bitcast(I32), w2_scales[0, 4 * q : 4 * q + 4, :].bitcast(I32))
 
         x_rows = xT.rearrange("(p j) t -> p j t", j=PACK)
-        planes = []
-        for j in range(PACK):
-            plane = keep.tile([P, T], F32, name="plane%d" % j)
-            nc.sync.dma_start(plane[:], x_rows[:, j, :])
-            planes.append(plane)
-            if j == 0:
-                nc.sync.dma_start(offsets[:], offs)
-
-        w1_rows = w1.rearrange("(p j) c -> p j c", j=PACK)
-        cols = H // W_PARTS
-        w1_raw = []
-        for h in range(W_PARTS):
-            raw = keep.tile([P, PACK, cols], F32, name="w1_raw%d" % h)
-            nc.sync.dma_start(raw[:], w1_rows[:, :, h * cols : (h + 1) * cols])
-            w1_raw.append(raw)
+        planes = [keep.tile([P, T], F32, name="plane%d" % j) for j in range(PACK)]
+        w1_raw = keep.tile([P, PACK, H], F32, name="w1_raw")
+        nc.sync.dma_start(planes[0][:], x_rows[:, 0, :])
+        nc.sync.dma_start(offsets[:], offs)
+        nc.sync.dma_start(w1_raw[:], w1.rearrange("(p j) c -> p j c", j=PACK))
+        for j in range(1, PACK - 1):
+            nc.sync.dma_start(planes[j][:], x_rows[:, j, :])
+        last = PACK - 1
+        pieces = [slice(a, b) for a, b in zip(CUTS[:-1], CUTS[1:])]
+        for cols in pieces:
+            nc.sync.dma_start(planes[last][:, cols], x_rows[:, last, cols])
         nc.sync.dma_start(w2_codes[:].bitcast(I32), w2_words[0].rearrange("p n t -> p (n t)").bitcast(I32))
 
-        picked = keep.tile([P, CHUNKS, 2, PAIRS, PACK], BF16, name="picked", align_bytes=64)
-        for j in range(PACK):
-            nc.vector.tensor_copy(
-                picked[:, :, :, :, j].rearrange("p c s n -> p s c n"),
-                planes[j][:].indirect(offsets[:]),
-            )
-
-        w1_grouped = keep.tile([P, PACK, P, PACK], BF16, name="w1_grouped", tag="shared", align_bytes=64)
-        ms = cols // PACK
-        for h in range(W_PARTS):
-            nc.scalar.copy(
-                w1_grouped[:, :, h * ms : (h + 1) * ms, :].rearrange("p t m j -> p m j t"),
-                w1_raw[h][:].rearrange("p j (m t) -> p m j t", t=PACK),
-            )
+        w1_grouped = keep.tile([P, PACK, P, PACK], BF16, name="w1_grouped", align_bytes=64)
+        nc.scalar.copy(
+            w1_grouped[:].rearrange("p t m j -> p m j t"),
+            w1_raw[:].rearrange("p j (m t) -> p m j t", t=PACK),
+        )
         w1_codes = keep.tile([P, H], U32, name="w1_codes", align_bytes=64)
         w1_plane = keep.tile([P, H], U8, name="w1_plane", align_bytes=64)
         nc.vector.quantize_mx(
             out=w1_codes[:].bitcast(FP8X4), scales=w1_plane[:], in_=w1_grouped[:].rearrange("p t m j -> p (t m j)")
         )
 
+        picked = [keep.tile([P, V, PACK], BF16, name="picked%d" % s, align_bytes=64) for s in range(2)]
+        lists = [offsets[:, s * (V // 16) : (s + 1) * (V // 16)] for s in range(2)]
+        for j in range(last):
+            for s in range(2):
+                nc.vector.tensor_copy(picked[s][:, :, j], planes[j][:].indirect(lists[s]))
+        rounded = keep.tile([P, T], BF16, name="rounded")
+        for i, cols in enumerate(pieces):
+            if i in ROUNDED_ON_VECTOR:
+                nc.vector.tensor_copy(rounded[:, cols], planes[last][:, cols])
+            else:
+                nc.scalar.activation(rounded[:, cols], planes[last][:, cols], ACT.Copy)
+        nc.vector.tensor_copy(picked[0][:, :, last], planes[last][:].indirect(lists[0]))
+        nc.scalar.activation(picked[1][:, :, last], rounded[:].indirect(lists[1]), ACT.Copy)
+
         warm = psum.tile([P, N], F32, name="warm", tag="bank%d_1" % (CHUNKS - 1))
         for i in range(WARM_PASSES):
             mx_pass(warm[:], w2_codes[:, :P], w2_plane[:, :P], w2_codes[:], w2_plane[:])
 
-        later_codes = keep.tile([P, CHUNKS, 2 * PAIRS], U32, name="later_codes", tag="shared", align_bytes=64)
-        first_codes = keep.tile([P, 2 * PAIRS], U32, name="first_codes", align_bytes=64)
-        hidden = []
-        for c in range(CHUNKS):
-            x_codes = first_codes[:] if c == 0 else later_codes[:, c, :]
-            x_plane = keep.tile([P, 2 * PAIRS], U8, name="x_plane%d" % c, align_bytes=64)
-            nc.vector.quantize_mx(
-                out=x_codes.bitcast(FP8X4), scales=x_plane[:], in_=picked[:, c].rearrange("p s n j -> p (s n j)")
-            )
-            sides = []
-            for s in range(2):
-                bank = psum.tile([P, PACK, PAIRS], F32, name="hidden%d_%d" % (c, s), tag="bank%d_%d" % (c, s))
-                tokens = slice(s * PAIRS, (s + 1) * PAIRS)
-                for t in range(PACK):
-                    channels = slice(t * P, (t + 1) * P)
-                    mx_pass(bank[:, t, :], w1_codes[:, channels], w1_plane[:, channels], x_codes[:, tokens], x_plane[:, tokens])
-                sides.append(bank)
-            hidden.append(sides)
+        x_codes = [keep.tile([P, V], U32, name="x_codes%d" % s, align_bytes=64) for s in range(2)]
+        x_plane = [keep.tile([P, V], U8, name="x_plane%d" % s, align_bytes=64) for s in range(2)]
+        for s in range(2):
+            for a, b in QCUTS:
+                nc.vector.quantize_mx(
+                    out=x_codes[s][:, a:b].bitcast(FP8X4), scales=x_plane[s][:, a:b], in_=picked[s][:, a:b, :].rearrange("p n j -> p (n j)")
+                )
+        hidden = [[None, None] for c in range(CHUNKS)]
+        for step in range(CHUNKS + 1):
+            for s, c in ((0, step), (1, step - 1)):
+                if 0 <= c < CHUNKS:
+                    tokens = slice(c * PAIRS, (c + 1) * PAIRS)
+                    bank = psum.tile([P, PACK, PAIRS], F32, name="hidden%d_%d" % (c, s), tag="bank%d_%d" % (c, s))
+                    for t in range(PACK):
+                        channels = slice(t * P, (t + 1) * P)
+                        mx_pass(bank[:, t, :], w1_codes[:, channels], w1_plane[:, channels], x_codes[s][:, tokens], x_plane[s][:, tokens])
+                    hidden[c][s] = bank
 
         firsts = []
         for c in range(CHUNKS):
@@ -151,5 +154,8 @@ def tile_picked_siam_abs_e_kernel(tc, xT, w1, w2_words, w2_scales, offs, out):
         for (c0, c1), halves in zip(GROUPS, results):
             staged = keep.tile([P, N // P, (c1 - c0) * PAIRS], F32, name="staged%d" % c0)
             nc.scalar.copy(staged[:, 0, :], halves[0][:])
-            nc.vector.tensor_copy(staged[:, 1, :], halves[1][:])
+            if c0 in OUT_ON_SCALAR:
+                nc.scalar.copy(staged[:, 1, :], halves[1][:])
+            else:
+                nc.vector.tensor_copy(staged[:, 1, :], halves[1][:])
             nc.sync.dma_start(out_rows[:, :, c0 * PAIRS : c1 * PAIRS], staged[:])

@@ -17,19 +17,35 @@ ACT = mybir.ActivationFunctionType
 
 P = 128
 PACK = 4
+SIDES = 2
 PAIRS = 128
 CHUNKS = V // PAIRS
-CUTS = (0, 1536, 2560, 3584, 4096)
-ROUNDED_ON_VECTOR = (2,)
-QCUTS = ((0, 128), (128, 256), (256, 512))
-OUT_ON_SCALAR = ()
-WARM_PASSES = 5
-ABS_ON_VECTOR = (0,)
-GROUPS = ((0, 1), (1, 2), (2, 3), (3, 4))
+ROW_TILES = N // P
+LIST_COLUMNS = V // 16
+
+LAST_SLOT_CUTS = (0, 2048, 3072, 4096)
+PIECE_ON_VECTOR = 1
+W1_HALF = H // 2
+QUANTISED_TOGETHER = ((0, 1), (1, 2), (2, 4))
+ABS_ON_VECTOR = 0
+WARM_UP_PASSES = 5
+
+
+def side_0_leads(count):
+    order = []
+    for step in range(count + 1):
+        if step < count:
+            order.append((0, step))
+        if step > 0:
+            order.append((1, step - 1))
+    return order
 
 
 def tile_picked_siam_abs_e_kernel(tc, xT, w1, w2_words, w2_scales, offs, out):
     nc = tc.nc
+
+    def quantise(codes, plane, values):
+        nc.vector.quantize_mx(out=codes.bitcast(FP8X4), scales=plane, in_=values)
 
     def mx_pass(acc, lhs_codes, lhs_plane, rhs_codes, rhs_plane):
         nc.tensor.matmul_mx(
@@ -54,108 +70,116 @@ def tile_picked_siam_abs_e_kernel(tc, xT, w1, w2_words, w2_scales, offs, out):
             nc.scalar.dma_start(w2_plane[32 * q : 32 * q + 4, :].bitcast(I32), w2_scales[0, 4 * q : 4 * q + 4, :].bitcast(I32))
 
         x_rows = xT.rearrange("(p j) t -> p j t", j=PACK)
-        planes = [keep.tile([P, T], F32, name="plane%d" % j) for j in range(PACK)]
-        w1_raw = keep.tile([P, PACK, H], F32, name="w1_raw")
-        nc.sync.dma_start(planes[0][:], x_rows[:, 0, :])
-        nc.sync.dma_start(offsets[:], offs)
-        nc.sync.dma_start(w1_raw[:], w1.rearrange("(p j) c -> p j c", j=PACK))
-        for j in range(1, PACK - 1):
-            nc.sync.dma_start(planes[j][:], x_rows[:, j, :])
+        slots = [keep.tile([P, T], F32, name="slot%d" % j) for j in range(PACK)]
         last = PACK - 1
-        pieces = [slice(a, b) for a, b in zip(CUTS[:-1], CUTS[1:])]
-        for cols in pieces:
-            nc.sync.dma_start(planes[last][:, cols], x_rows[:, last, cols])
+        nc.sync.dma_start(slots[0][:], x_rows[:, 0, :])
+        nc.sync.dma_start(offsets[:], offs)
+        for j in range(1, last):
+            nc.sync.dma_start(slots[j][:], x_rows[:, j, :])
+        pieces = [slice(a, b) for a, b in zip(LAST_SLOT_CUTS[:-1], LAST_SLOT_CUTS[1:])]
+        for samples in pieces:
+            nc.sync.dma_start(slots[last][:, samples], x_rows[:, last, samples])
+        w1_rows = w1.rearrange("(p j) c -> p j c", j=PACK)
+        w1_raw = []
+        for start in range(0, H, W1_HALF):
+            raw = keep.tile([P, PACK, W1_HALF], F32, name="w1_raw%d" % start)
+            nc.sync.dma_start(raw[:], w1_rows[:, :, start : start + W1_HALF])
+            w1_raw.append(raw)
         nc.sync.dma_start(w2_codes[:].bitcast(I32), w2_words[0].rearrange("p n t -> p (n t)").bitcast(I32))
 
-        w1_grouped = keep.tile([P, PACK, P, PACK], BF16, name="w1_grouped", align_bytes=64)
-        nc.scalar.copy(
-            w1_grouped[:].rearrange("p t m j -> p m j t"),
-            w1_raw[:].rearrange("p j (m t) -> p m j t", t=PACK),
-        )
-        w1_codes = keep.tile([P, H], U32, name="w1_codes", align_bytes=64)
-        w1_plane = keep.tile([P, H], U8, name="w1_plane", align_bytes=64)
-        nc.vector.quantize_mx(
-            out=w1_codes[:].bitcast(FP8X4), scales=w1_plane[:], in_=w1_grouped[:].rearrange("p t m j -> p (t m j)")
-        )
-
-        picked = [keep.tile([P, V, PACK], BF16, name="picked%d" % s, align_bytes=64) for s in range(2)]
-        lists = [offsets[:, s * (V // 16) : (s + 1) * (V // 16)] for s in range(2)]
+        picked = [keep.tile([P, V, PACK], BF16, name="picked%d" % s, align_bytes=64) for s in range(SIDES)]
+        lists = [offsets[:, s * LIST_COLUMNS : (s + 1) * LIST_COLUMNS] for s in range(SIDES)]
         for j in range(last):
-            for s in range(2):
-                nc.vector.tensor_copy(picked[s][:, :, j], planes[j][:].indirect(lists[s]))
+            for s in range(SIDES):
+                nc.vector.tensor_copy(picked[s][:, :, j], slots[j][:].indirect(lists[s]))
         rounded = keep.tile([P, T], BF16, name="rounded")
-        for i, cols in enumerate(pieces):
-            if i in ROUNDED_ON_VECTOR:
-                nc.vector.tensor_copy(rounded[:, cols], planes[last][:, cols])
+        for i, samples in enumerate(pieces):
+            if i == PIECE_ON_VECTOR:
+                nc.vector.tensor_copy(rounded[:, samples], slots[last][:, samples])
             else:
-                nc.scalar.activation(rounded[:, cols], planes[last][:, cols], ACT.Copy)
-        nc.vector.tensor_copy(picked[0][:, :, last], planes[last][:].indirect(lists[0]))
+                nc.scalar.activation(rounded[:, samples], slots[last][:, samples], ACT.Copy)
+        nc.vector.tensor_copy(picked[0][:, :, last], slots[last][:].indirect(lists[0]))
         nc.scalar.activation(picked[1][:, :, last], rounded[:].indirect(lists[1]), ACT.Copy)
 
-        warm = psum.tile([P, N], F32, name="warm", tag="bank%d_1" % (CHUNKS - 1))
-        for i in range(WARM_PASSES):
-            mx_pass(warm[:], w2_codes[:, :P], w2_plane[:, :P], w2_codes[:], w2_plane[:])
+        warm_up = psum.tile([P, N], F32, name="warm_up", tag="bank%d_1" % (CHUNKS - 1))
+        for repeat in range(WARM_UP_PASSES):
+            mx_pass(warm_up[:], w2_codes[:, :P], w2_plane[:, :P], w2_codes[:], w2_plane[:])
 
-        x_codes = [keep.tile([P, V], U32, name="x_codes%d" % s, align_bytes=64) for s in range(2)]
-        x_plane = [keep.tile([P, V], U8, name="x_plane%d" % s, align_bytes=64) for s in range(2)]
-        for s in range(2):
-            for a, b in QCUTS:
-                nc.vector.quantize_mx(
-                    out=x_codes[s][:, a:b].bitcast(FP8X4), scales=x_plane[s][:, a:b], in_=picked[s][:, a:b, :].rearrange("p n j -> p (n j)")
-                )
-        hidden = [[None, None] for c in range(CHUNKS)]
-        for step in range(CHUNKS + 1):
-            for s, c in ((0, step), (1, step - 1)):
-                if 0 <= c < CHUNKS:
-                    tokens = slice(c * PAIRS, (c + 1) * PAIRS)
-                    bank = psum.tile([P, PACK, PAIRS], F32, name="hidden%d_%d" % (c, s), tag="bank%d_%d" % (c, s))
-                    for t in range(PACK):
-                        channels = slice(t * P, (t + 1) * P)
-                        mx_pass(bank[:, t, :], w1_codes[:, channels], w1_plane[:, channels], x_codes[s][:, tokens], x_plane[s][:, tokens])
-                    hidden[c][s] = bank
-
-        firsts = []
-        for c in range(CHUNKS):
-            first = keep.tile([P, PAIRS, PACK], F32, name="first%d" % c)
-            nc.scalar.activation(first[:], hidden[c][0][:].rearrange("p t n -> p n t"), ACT.Relu)
-            firsts.append(first)
-        diffs = []
-        for c in range(CHUNKS):
-            diff = keep.tile([P, PAIRS, PACK], BF16, name="diff%d" % c)
-            nc.vector.scalar_tensor_tensor(
-                out=diff[:], in0=hidden[c][1][:].rearrange("p t n -> p n t"), scalar=0.0, in1=firsts[c][:], op0=ALU.max, op1=ALU.subtract
+        w1_dealt = keep.tile([P, PACK, P, PACK], BF16, name="w1_dealt", tag="w1_dealt_then_codes", align_bytes=64)
+        half = W1_HALF // PACK
+        for h, raw in enumerate(w1_raw):
+            nc.vector.tensor_copy(
+                w1_dealt[:, :, h * half : (h + 1) * half, :].rearrange("p t m j -> p m j t"),
+                raw[:].rearrange("p j (m t) -> p m j t", t=PACK),
             )
-            diffs.append(diff)
+        w1_codes = keep.tile([P, H], U32, name="w1_codes", align_bytes=64)
+        w1_plane = keep.tile([P, H], U8, name="w1_plane", align_bytes=64)
+        quantise(w1_codes[:], w1_plane[:], w1_dealt[:].rearrange("p t m j -> p (t m j)"))
+
+        first_codes = keep.tile([P, PAIRS], U32, name="first_codes", align_bytes=64)
+        later_codes = keep.tile([P, SIDES, V], U32, name="later_codes", tag="w1_dealt_then_codes", align_bytes=64)
+        x_plane = [keep.tile([P, V], U8, name="x_plane%d" % s, align_bytes=64) for s in range(SIDES)]
+
+        def x_codes(s, pairs):
+            return first_codes[:] if (s, pairs.start) == (0, 0) else later_codes[:, s, pairs]
+
+        for s, run in side_0_leads(len(QUANTISED_TOGETHER)):
+            c0, c1 = QUANTISED_TOGETHER[run]
+            pairs = slice(c0 * PAIRS, c1 * PAIRS)
+            quantise(x_codes(s, pairs), x_plane[s][:, pairs], picked[s][:, pairs, :].rearrange("p v j -> p (v j)"))
+
+        hidden = [[None] * SIDES for c in range(CHUNKS)]
+        for s, c in side_0_leads(CHUNKS):
+            pairs = slice(c * PAIRS, (c + 1) * PAIRS)
+            bank = psum.tile([P, PACK, PAIRS], F32, name="hidden%d_%d" % (c, s), tag="bank%d_%d" % (c, s))
+            for t in range(PACK):
+                channels = slice(t * P, (t + 1) * P)
+                mx_pass(bank[:, t, :], w1_codes[:, channels], w1_plane[:, channels], x_codes(s, pairs), x_plane[s][:, pairs])
+            hidden[c][s] = bank
+
+        relu_0 = []
+        for c in range(CHUNKS):
+            values = keep.tile([P, PAIRS, PACK], F32, name="relu_0_%d" % c)
+            nc.scalar.activation(values[:], hidden[c][0][:].rearrange("p t v -> p v t"), ACT.Relu)
+            relu_0.append(values)
+        differences = []
+        for c in range(CHUNKS):
+            difference = keep.tile([P, PAIRS, PACK], BF16, name="difference%d" % c)
+            nc.vector.scalar_tensor_tensor(
+                out=difference[:],
+                in0=hidden[c][1][:].rearrange("p t v -> p v t"),
+                scalar=0.0,
+                in1=relu_0[c][:],
+                op0=ALU.max,
+                op1=ALU.subtract,
+            )
+            differences.append(difference)
         z = keep.tile([P, CHUNKS, PAIRS * PACK], BF16, name="z", align_bytes=64)
         for c in range(CHUNKS):
-            flat = diffs[c][:].rearrange("p n t -> p (n t)")
-            if c in ABS_ON_VECTOR:
-                negated = keep.tile([P, PAIRS * PACK], BF16, name="negated%d" % c)
-                nc.vector.tensor_scalar(out=negated[:], in0=flat, scalar1=-1.0, scalar2=None, op0=ALU.mult)
-                nc.vector.tensor_tensor(out=z[:, c, :], in0=flat, in1=negated[:], op=ALU.max)
+            signed = differences[c][:].rearrange("p v t -> p (v t)")
+            if c == ABS_ON_VECTOR:
+                negated = keep.tile([P, PAIRS * PACK], BF16, name="negated")
+                nc.vector.tensor_scalar(out=negated[:], in0=signed, scalar1=-1.0, scalar2=None, op0=ALU.mult)
+                nc.vector.tensor_tensor(out=z[:, c, :], in0=signed, in1=negated[:], op=ALU.max)
             else:
-                nc.scalar.activation(z[:, c, :], flat, ACT.Abs)
+                nc.scalar.activation(z[:, c, :], signed, ACT.Abs)
 
         results = []
-        for c0, c1 in GROUPS:
-            width = (c1 - c0) * PAIRS
-            z_codes = keep.tile([P, width], U32, name="z_codes%d" % c0, align_bytes=64)
-            z_plane = keep.tile([P, width], U8, name="z_plane%d" % c0, align_bytes=64)
-            nc.vector.quantize_mx(out=z_codes[:].bitcast(FP8X4), scales=z_plane[:], in_=z[:, c0:c1, :].rearrange("p c e -> p (c e)"))
-            halves = []
-            for r in range(N // P):
-                result = psum.tile([P, width], F32, name="result%d_%d" % (c0, r), tag="bank%d_%d" % (c0, r))
+        for c in range(CHUNKS):
+            z_codes = keep.tile([P, PAIRS], U32, name="z_codes%d" % c, align_bytes=64)
+            z_plane = keep.tile([P, PAIRS], U8, name="z_plane%d" % c, align_bytes=64)
+            quantise(z_codes[:], z_plane[:], z[:, c, :])
+            banks = []
+            for r in range(ROW_TILES):
+                bank = psum.tile([P, PAIRS], F32, name="result%d_%d" % (c, r), tag="bank%d_%d" % (c, r))
                 rows = slice(r * P, (r + 1) * P)
-                mx_pass(result[:], w2_codes[:, rows], w2_plane[:, rows], z_codes[:], z_plane[:])
-                halves.append(result)
-            results.append(halves)
+                mx_pass(bank[:], w2_codes[:, rows], w2_plane[:, rows], z_codes[:], z_plane[:])
+                banks.append(bank)
+            results.append(banks)
 
         out_rows = out.rearrange("(r p) v -> p r v", p=P)
-        for (c0, c1), halves in zip(GROUPS, results):
-            staged = keep.tile([P, N // P, (c1 - c0) * PAIRS], F32, name="staged%d" % c0)
-            nc.scalar.copy(staged[:, 0, :], halves[0][:])
-            if c0 in OUT_ON_SCALAR:
-                nc.scalar.copy(staged[:, 1, :], halves[1][:])
-            else:
-                nc.vector.tensor_copy(staged[:, 1, :], halves[1][:])
-            nc.sync.dma_start(out_rows[:, :, c0 * PAIRS : c1 * PAIRS], staged[:])
+        for c, banks in enumerate(results):
+            staged = keep.tile([P, ROW_TILES, PAIRS], F32, name="staged%d" % c)
+            nc.scalar.copy(staged[:, 0, :], banks[0][:])
+            nc.vector.tensor_copy(staged[:, 1, :], banks[1][:])
+            nc.sync.dma_start(out_rows[:, :, c * PAIRS : (c + 1) * PAIRS], staged[:])

from contextlib import ExitStack

import concourse.mybir as mybir

K, T, S, V, H, N = 512, 4096, 1024, 512, 512, 256
FLOPS = 2 * K * H * S + 2 * H * N * V

F32 = mybir.dt.float32
BF16 = mybir.dt.bfloat16
I32 = mybir.dt.int32
U32 = mybir.dt.uint32
U16 = mybir.dt.uint16
U8 = mybir.dt.uint8
FP8X4 = mybir.dt.float8_e4m3fn_x4
ALU = mybir.AluOpType
ACT = mybir.ActivationFunctionType

P = 128
PACK = 4
SIDES = 2
PAIRS = 128
CHUNKS = V // PAIRS
ROW_TILES = N // P
LIST_COLUMNS = V // 16

LAST_SLOT_CUTS = (0, 2048, 3072, 4096)
PIECE_ON_VECTOR = 1
W1_HALF = H // 2
QUANTISED_TOGETHER = ((0, 1), (1, 2), (2, 4))
ABS_ON_VECTOR = 0
WARM_UP_PASSES = 5


def side_0_leads(count):
    order = []
    for step in range(count + 1):
        if step < count:
            order.append((0, step))
        if step > 0:
            order.append((1, step - 1))
    return order


def tile_picked_siam_abs_e_kernel(tc, xT, w1, w2_words, w2_scales, offs, out):
    nc = tc.nc

    def quantise(codes, plane, values):
        nc.vector.quantize_mx(out=codes.bitcast(FP8X4), scales=plane, in_=values)

    def mx_pass(acc, lhs_codes, lhs_plane, rhs_codes, rhs_plane):
        nc.tensor.matmul_mx(
            out=acc,
            lhsT=lhs_codes.bitcast(FP8X4),
            lhsT_scale=lhs_plane,
            rhs=rhs_codes.bitcast(FP8X4),
            rhs_scale=rhs_plane,
            start=True,
            stop=True,
        )

    with ExitStack() as ctx:
        keep = ctx.enter_context(tc.tile_pool(name="keep", bufs=1))
        psum = ctx.enter_context(tc.psum_pool(name="psum", bufs=1))

        offsets = keep.tile([P, S // 16], U16, name="offsets")
        w2_codes = keep.tile([P, N], U32, name="w2_codes", align_bytes=64)
        w2_plane = keep.tile([P, N], U8, name="w2_plane", align_bytes=64)
        nc.gpsimd.memset(w2_plane[:].bitcast(I32), 0)
        for q in range(4):
            nc.scalar.dma_start(w2_plane[32 * q : 32 * q + 4, :].bitcast(I32), w2_scales[0, 4 * q : 4 * q + 4, :].bitcast(I32))

        x_rows = xT.rearrange("(p j) t -> p j t", j=PACK)
        slots = [keep.tile([P, T], F32, name="slot%d" % j) for j in range(PACK)]
        last = PACK - 1
        nc.sync.dma_start(slots[0][:], x_rows[:, 0, :])
        nc.sync.dma_start(offsets[:], offs)
        for j in range(1, last):
            nc.sync.dma_start(slots[j][:], x_rows[:, j, :])
        pieces = [slice(a, b) for a, b in zip(LAST_SLOT_CUTS[:-1], LAST_SLOT_CUTS[1:])]
        for samples in pieces:
            nc.sync.dma_start(slots[last][:, samples], x_rows[:, last, samples])
        w1_rows = w1.rearrange("(p j) c -> p j c", j=PACK)
        w1_raw = []
        for start in range(0, H, W1_HALF):
            raw = keep.tile([P, PACK, W1_HALF], F32, name="w1_raw%d" % start)
            nc.sync.dma_start(raw[:], w1_rows[:, :, start : start + W1_HALF])
            w1_raw.append(raw)
        nc.sync.dma_start(w2_codes[:].bitcast(I32), w2_words[0].rearrange("p n t -> p (n t)").bitcast(I32))

        picked = [keep.tile([P, V, PACK], BF16, name="picked%d" % s, align_bytes=64) for s in range(SIDES)]
        lists = [offsets[:, s * LIST_COLUMNS : (s + 1) * LIST_COLUMNS] for s in range(SIDES)]
        for j in range(last):
            for s in range(SIDES):
                nc.vector.tensor_copy(picked[s][:, :, j], slots[j][:].indirect(lists[s]))
        rounded = keep.tile([P, T], BF16, name="rounded")
        for i, samples in enumerate(pieces):
            if i == PIECE_ON_VECTOR:
                nc.vector.tensor_copy(rounded[:, samples], slots[last][:, samples])
            else:
                nc.scalar.activation(rounded[:, samples], slots[last][:, samples], ACT.Copy)
        nc.vector.tensor_copy(picked[0][:, :, last], slots[last][:].indirect(lists[0]))
        nc.scalar.activation(picked[1][:, :, last], rounded[:].indirect(lists[1]), ACT.Copy)

        warm_up = psum.tile([P, N], F32, name="warm_up", tag="bank%d_1" % (CHUNKS - 1))
        for repeat in range(WARM_UP_PASSES):
            mx_pass(warm_up[:], w2_codes[:, :P], w2_plane[:, :P], w2_codes[:], w2_plane[:])

        w1_dealt = keep.tile([P, PACK, P, PACK], BF16, name="w1_dealt", tag="w1_dealt_then_codes", align_bytes=64)
        half = W1_HALF // PACK
        for h, raw in enumerate(w1_raw):
            nc.vector.tensor_copy(
                w1_dealt[:, :, h * half : (h + 1) * half, :].rearrange("p t m j -> p m j t"),
                raw[:].rearrange("p j (m t) -> p m j t", t=PACK),
            )
        w1_codes = keep.tile([P, H], U32, name="w1_codes", align_bytes=64)
        w1_plane = keep.tile([P, H], U8, name="w1_plane", align_bytes=64)
        quantise(w1_codes[:], w1_plane[:], w1_dealt[:].rearrange("p t m j -> p (t m j)"))

        first_codes = keep.tile([P, PAIRS], U32, name="first_codes", align_bytes=64)
        later_codes = keep.tile([P, SIDES, V], U32, name="later_codes", tag="w1_dealt_then_codes", align_bytes=64)
        x_plane = [keep.tile([P, V], U8, name="x_plane%d" % s, align_bytes=64) for s in range(SIDES)]

        def x_codes(s, pairs):
            return first_codes[:] if (s, pairs.start) == (0, 0) else later_codes[:, s, pairs]

        for s, run in side_0_leads(len(QUANTISED_TOGETHER)):
            c0, c1 = QUANTISED_TOGETHER[run]
            pairs = slice(c0 * PAIRS, c1 * PAIRS)
            quantise(x_codes(s, pairs), x_plane[s][:, pairs], picked[s][:, pairs, :].rearrange("p v j -> p (v j)"))

        hidden = [[None] * SIDES for c in range(CHUNKS)]
        for s, c in side_0_leads(CHUNKS):
            pairs = slice(c * PAIRS, (c + 1) * PAIRS)
            bank = psum.tile([P, PACK, PAIRS], F32, name="hidden%d_%d" % (c, s), tag="bank%d_%d" % (c, s))
            for t in range(PACK):
                channels = slice(t * P, (t + 1) * P)
                mx_pass(bank[:, t, :], w1_codes[:, channels], w1_plane[:, channels], x_codes(s, pairs), x_plane[s][:, pairs])
            hidden[c][s] = bank

        relu_0 = []
        for c in range(CHUNKS):
            values = keep.tile([P, PAIRS, PACK], F32, name="relu_0_%d" % c)
            nc.scalar.activation(values[:], hidden[c][0][:].rearrange("p t v -> p v t"), ACT.Relu)
            relu_0.append(values)
        differences = []
        for c in range(CHUNKS):
            difference = keep.tile([P, PAIRS, PACK], BF16, name="difference%d" % c)
            nc.vector.scalar_tensor_tensor(
                out=difference[:],
                in0=hidden[c][1][:].rearrange("p t v -> p v t"),
                scalar=0.0,
                in1=relu_0[c][:],
                op0=ALU.max,
                op1=ALU.subtract,
            )
            differences.append(difference)
        z = keep.tile([P, CHUNKS, PAIRS * PACK], BF16, name="z", align_bytes=64)
        for c in range(CHUNKS):
            signed = differences[c][:].rearrange("p v t -> p (v t)")
            if c == ABS_ON_VECTOR:
                negated = keep.tile([P, PAIRS * PACK], BF16, name="negated")
                nc.vector.tensor_scalar(out=negated[:], in0=signed, scalar1=-1.0, scalar2=None, op0=ALU.mult)
                nc.vector.tensor_tensor(out=z[:, c, :], in0=signed, in1=negated[:], op=ALU.max)
            else:
                nc.scalar.activation(z[:, c, :], signed, ACT.Abs)

        results = []
        for c in range(CHUNKS):
            z_codes = keep.tile([P, PAIRS], U32, name="z_codes%d" % c, align_bytes=64)
            z_plane = keep.tile([P, PAIRS], U8, name="z_plane%d" % c, align_bytes=64)
            quantise(z_codes[:], z_plane[:], z[:, c, :])
            banks = []
            for r in range(ROW_TILES):
                bank = psum.tile([P, PAIRS], F32, name="result%d_%d" % (c, r), tag="bank%d_%d" % (c, r))
                rows = slice(r * P, (r + 1) * P)
                mx_pass(bank[:], w2_codes[:, rows], w2_plane[:, rows], z_codes[:], z_plane[:])
                banks.append(bank)
            results.append(banks)

        out_rows = out.rearrange("(r p) v -> p r v", p=P)
        for c, banks in enumerate(results):
            staged = keep.tile([P, ROW_TILES, PAIRS], F32, name="staged%d" % c)
            nc.scalar.copy(staged[:, 0, :], banks[0][:])
            nc.vector.tensor_copy(staged[:, 1, :], banks[1][:])
            nc.sync.dma_start(out_rows[:, :, c * PAIRS : (c + 1) * PAIRS], staged[:])
